import numpy as np
import ml_dtypes


def mxq(x, axis, fmt="e4m3"):
    dtype, down = {"e4m3": (ml_dtypes.float8_e4m3fn, 7), "e5m2": (ml_dtypes.float8_e5m2, 14)}[fmt]
    v = np.moveaxis(np.asarray(x, np.float32).astype(ml_dtypes.bfloat16).astype(np.float64), axis, -1)
    blocks = v.reshape(v.shape[:-1] + (-1, 32))
    amax = np.abs(blocks).max(-1, keepdims=True)
    byte = np.maximum(np.where(amax > 0, np.frexp(amax)[1] - 1 + 127, 0) - down, 1)
    scale = np.exp2(byte - 127.0)
    codes = (blocks / scale).astype(np.float32).astype(dtype).astype(np.float64)
    return np.moveaxis((codes * scale).reshape(v.shape), -1, axis)


WIDE = False


def mx_kscale(k):
    if not WIDE:
        return np.ones(k)
    levels = np.array([10, -10, 5, -5, 0])
    if k % 512:
        return np.exp2(np.random.permutation(np.resize(levels, k // 32))).repeat(32)
    a = np.empty((k // 512, 16))
    for p in range(k // 512):
        a[p, :8] = np.random.permutation(np.resize(levels, 8))
        for g in range(8):
            far = levels[np.abs(levels - a[p, g]) >= 10]
            a[p, g + 8] = far[np.random.randint(len(far))]
    return np.exp2(a.ravel()).repeat(32)


def f64(x):
    return np.asarray(x).astype(np.float64)


def striped(idx):
    return np.tile(idx.reshape(-1, 16).T, (8, 1)).astype(np.uint16)


def unstriped(offs):
    return offs[:16].T.reshape(-1).astype(np.int64)


def striped8(idx):
    return np.concatenate([x.reshape(-1, 16).T for x in idx]).astype(np.uint16)


def runs(offs, k):
    lists = np.stack([offs[16 * r : 16 * r + 16].T.reshape(-1) for r in range(8)]).astype(np.int64)
    return lists[np.arange(k) % 512 // 64]


def pack_weight(w):
    k, n = w.shape
    w = f64(np.asarray(w, np.float32).astype(ml_dtypes.bfloat16)).reshape(k // 32, 32, n)
    amax = np.abs(w).max(1)
    byte = np.clip(np.where(amax > 0, np.frexp(amax)[1] - 1 + 127 - 7, 1), 1, 254)
    scaled = (w * np.exp2(127.0 - byte)[:, None, :]).reshape(k, n).astype(np.float32)
    words = np.ascontiguousarray(scaled.reshape(k // 512, 128, 4, n).transpose(0, 1, 3, 2)).astype(ml_dtypes.float8_e4m3fn).view(np.uint8)
    return words, np.ascontiguousarray(byte.astype(np.uint8).reshape(k // 512, 16, n))


def unpack_weight(words, scales):
    g, p, n, _ = words.shape
    vals = np.ascontiguousarray(words).view(ml_dtypes.float8_e4m3fn).astype(np.float64) * np.repeat(np.exp2(scales.astype(np.float64) - 127.0), 8, axis=1)[..., None]
    return vals.transpose(0, 1, 3, 2).reshape(g * 512, n)


def sigmoid(v):
    return 1.0 / (1.0 + np.exp(-np.maximum(v, -700.0)))


K, T, S, H, C, W = 512, 2048, 512, 512, 512, 2048


def setup_inputs():
    n = np.random.standard_normal
    s = mx_kscale(K)[:, None]
    packed_xT = pack_weight(n((K, T)) * s)
    return {
        "x_words": packed_xT[0],
        "x_scales": packed_xT[1],
        "w1": (n((K, H)) / np.sqrt(K) / s).astype(np.float32),
        "sl": np.random.uniform(1.0, 2.0, (H, 1)).astype(np.float32),
        "th": (0.5 * n((H, 1))).astype(np.float32),
        "gs": (np.random.uniform(0.5, 1.5, (K, 1)) / s).astype(np.float32),
        "offs": striped(np.random.permutation(T)[:S]),
        "n1": striped8(np.stack([np.random.permutation(S) for _ in range(8)])),
        "n2": striped8(np.stack([np.random.permutation(S) for _ in range(8)])),
        "cand": striped(np.random.permutation(T)[:C]),
        "n3": striped(np.random.randint(0, S, W)),
    }


def reference(x_words, x_scales, w1, sl, th, gs, offs, n1, n2, cand, n3):
    x_cand = unpack_weight(x_words, x_scales)[:, unstriped(cand)]
    xq = unpack_weight(x_words, x_scales)[:, unstriped(offs)]
    y = mxq(f64(w1), 0, "e4m3").T @ xq
    st = y - (y[np.arange(H)[:, None], runs(n1, H)])
    sg = sigmoid(f64(sl) * (st[np.arange(H)[:, None], runs(n2, H)] - f64(th)))
    z = f64(gs) * (y * sg)
    s = 0.0625 * ((x_cand.T @ mxq(z, 0, "e4m3")))
    mb = s[:, unstriped(n3)]
    sq = (mb) ** 2
    qs = sq.reshape(C, S, 4).sum(axis=2)
    return s / np.sqrt(qs + 0.5)

@@ -1,0 +1,197 @@
+from contextlib import ExitStack
+
+import concourse.mybir as mybir
+
+K, T, S, H, C, W = 512, 2048, 512, 512, 512, 2048
+FLOPS = 2 * K * H * S + 2 * K * C * S
+
+F32 = mybir.dt.float32
+BF16 = mybir.dt.bfloat16
+I32 = mybir.dt.int32
+U32 = mybir.dt.uint32
+U16 = mybir.dt.uint16
+U8 = mybir.dt.uint8
+FP8X4 = mybir.dt.float8_e4m3fn_x4
+ACT = mybir.ActivationFunctionType
+MULT = mybir.AluOpType.mult
+ADD = mybir.AluOpType.add
+
+P = 128
+PACK = 4
+HALF = 256
+MEMBERS = 4
+
+
+def column_pieces(first, last, most):
+    count = -(-(last - first) // most)
+    pairs = (last - first) // 2
+    cuts = [first + 2 * (pairs * i // count) for i in range(count + 1)]
+    return list(zip(cuts[:-1], cuts[1:]))
+
+
+def tile_picked_candehqgvar_none_p_kernel(tc, x_words, x_scales, w1, sl, th, gs, offs, n1, n2, cand, n3, out):
+    nc = tc.nc
+    with ExitStack() as ctx:
+        lists = ctx.enter_context(tc.tile_pool(name="lists", bufs=1))
+        keep = ctx.enter_context(tc.tile_pool(name="keep", bufs=1))
+        psum = ctx.enter_context(tc.psum_pool(name="psum", bufs=1))
+
+        offs_t = lists.tile([P, S // 16], U16, name="offs_t")
+        cand_t = lists.tile([P, C // 16], U16, name="cand_t")
+        n1_t = lists.tile([P, S // 16], U16, name="n1_t")
+        n2_t = lists.tile([P, S // 16], U16, name="n2_t")
+        n3_t = lists.tile([P, W // 16], U16, name="n3_t")
+
+        table_scales = keep.tile([P, T], U8, name="table_scales", align_bytes=64)
+        table_words = keep.tile([P, T], I32, name="table_words", align_bytes=64)
+        nc.vector.memset(table_scales[:].bitcast(I32), 0)
+
+        w_rows = w1.rearrange("(p j) c -> p j c", j=PACK)
+        w_raw = [keep.tile([P, PACK, HALF], F32, name=f"w_raw{h}", align_bytes=64) for h in range(2)]
+        nc.sync.dma_start(w_raw[0][:], w_rows[:, :, 0:HALF])
+        nc.sync.dma_start(offs_t[:], offs)
+        nc.sync.dma_start(cand_t[:], cand)
+        for q in range(4):
+            nc.sync.dma_start(
+                table_scales[32 * q : 32 * q + 4, :].bitcast(I32), x_scales[0, 4 * q : 4 * q + 4, :].bitcast(I32)
+            )
+        nc.sync.dma_start(w_raw[1][:], w_rows[:, :, HALF:H])
+        nc.sync.dma_start(table_words[:], x_words[0].rearrange("p n t -> p (n t)").bitcast(I32))
+        nc.sync.dma_start(n1_t[:], n1)
+        nc.sync.dma_start(n2_t[:], n2)
+        nc.sync.dma_start(n3_t[:], n3)
+
+        sl_t = keep.tile([P, PACK], F32, name="sl_t")
+        th_t = keep.tile([P, PACK], F32, name="th_t")
+        gs_t = keep.tile([P, PACK], F32, name="gs_t")
+        bias_t = keep.tile([P, PACK], F32, name="bias_t")
+        for tile, vec in ((sl_t, sl), (th_t, th), (gs_t, gs)):
+            nc.gpsimd.dma_start(tile[:], vec.rearrange("(p t) o -> p (t o)", t=PACK))
+        neg_sl = keep.tile([P, PACK], F32, name="neg_sl")
+        nc.gpsimd.tensor_scalar(neg_sl[:], sl_t[:], -1.0, 0.0, MULT, ADD)
+        nc.gpsimd.tensor_tensor(bias_t[:], neg_sl[:], th_t[:], MULT)
+
+        q_scales = keep.tile([P, S], U8, name="q_scales", align_bytes=64)
+        c_scales = keep.tile([P, C], U8, name="c_scales", align_bytes=64)
+        q_words = keep.tile([P, S], U32, name="q_words", align_bytes=64)
+        c_words = keep.tile([P, C], U32, name="c_words", align_bytes=64)
+        nc.vector.tensor_copy(q_scales[:], table_scales[:].indirect(offs_t[:]))
+        nc.vector.tensor_copy(c_scales[:], table_scales[:].indirect(cand_t[:]))
+
+        w_bf = keep.tile([P, PACK, P, PACK], BF16, name="w_bf", align_bytes=64)
+        for h in range(2):
+            nc.scalar.copy(
+                w_bf[:, :, 64 * h : 64 * h + 64, :].rearrange("p t m j -> p m j t"),
+                w_raw[h][:].rearrange("p j (m t) -> p m j t", t=PACK),
+            )
+        w_codes = keep.tile([P, H], U32, name="w_codes", align_bytes=64)
+        w_scales = keep.tile([P, H], U8, name="w_scales", align_bytes=64)
+        nc.vector.quantize_mx(w_codes[:].bitcast(FP8X4), w_scales[:], w_bf[:].rearrange("p t m j -> p (t m j)"))
+
+        nc.vector.tensor_copy(q_words[:], table_words[:].bitcast(U32).indirect(offs_t[:]))
+        nc.vector.tensor_copy(c_words[:], table_words[:].bitcast(U32).indirect(cand_t[:]))
+
+        y_ps = [psum.tile([P, S], F32, name=f"y_ps{t}") for t in range(PACK)]
+        y_sb = [keep.tile([P, S], F32, name=f"y_sb{t}") for t in range(PACK)]
+        y_neg = [keep.tile([P, S], F32, name=f"y_neg{t}") for t in range(PACK)]
+        st = [keep.tile([P, S], F32, name=f"st{t}") for t in range(PACK)]
+        sg = [keep.tile([P, S], F32, name=f"sg{t}") for t in range(PACK)]
+        z_f32 = [keep.tile([P, PACK, HALF], F32, name=f"z_f32{h}") for h in range(2)]
+        for t in range(PACK):
+            cols = slice(P * t, P * t + P)
+            nc.tensor.matmul_mx(
+                y_ps[t][:], lhsT=w_codes[:, cols].bitcast(FP8X4), lhsT_scale=w_scales[:, cols],
+                rhs=q_words[:].bitcast(FP8X4), rhs_scale=q_scales[:], start=True, stop=True,
+            )
+            nc.scalar.copy(y_sb[t][:], y_ps[t][:])
+        for t in range(PACK):
+            nc.vector.tensor_scalar(y_neg[t][:], y_sb[t][:], -1.0, None, MULT)
+            for h in range(2):
+                cols = slice(HALF * h, HALF * h + HALF)
+                nc.vector.tensor_tensor(
+                    st[t][:, cols], y_neg[t][:].indirect(n1_t[:, 16 * h : 16 * h + 16]), y_sb[t][:, cols], ADD
+                )
+            for h in range(2):
+                cols = slice(HALF * h, HALF * h + HALF)
+                nc.scalar.activation(
+                    sg[t][:, cols], st[t][:].indirect(n2_t[:, 16 * h : 16 * h + 16]), ACT.Sigmoid,
+                    bias=bias_t[:, t : t + 1], scale=sl_t[:, t : t + 1],
+                )
+        z_codes = []
+        z_scales = []
+        for h in range(2):
+            cols = slice(HALF * h, HALF * h + HALF)
+            for t in range(PACK):
+                nc.vector.scalar_tensor_tensor(
+                    z_f32[h][:, t, :], y_ps[t][:, cols], gs_t[:, t : t + 1], sg[t][:, cols], MULT, MULT
+                )
+            z_bf = keep.tile([P, HALF, PACK], BF16, name=f"z_bf{h}", align_bytes=64)
+            nc.vector.tensor_copy(
+                z_bf[:].rearrange("p (c i) t -> p c t i", i=4), z_f32[h][:].rearrange("p t (c i) -> p c t i", i=4)
+            )
+            codes = keep.tile([P, HALF], U32, name=f"z_codes{h}", align_bytes=64)
+            scales = keep.tile([P, HALF], U8, name=f"z_scales{h}", align_bytes=64)
+            nc.vector.quantize_mx(codes[:].bitcast(FP8X4), scales[:], z_bf[:].rearrange("p c t -> p (c t)"))
+            z_codes.append(codes)
+            z_scales.append(scales)
+
+        s_ps = [psum.tile([P, S], F32, name=f"s_ps{c}") for c in range(4)]
+        sq = [keep.tile([P, S], F32, name=f"sq{c}") for c in range(4)]
+        for h in range(2):
+            for c in range(4):
+                cols = slice(P * c, P * c + P)
+                nc.tensor.matmul_mx(
+                    s_ps[c][:, HALF * h : HALF * h + HALF], lhsT=c_words[:, cols].bitcast(FP8X4),
+                    lhsT_scale=c_scales[:, cols], rhs=z_codes[h][:].bitcast(FP8X4), rhs_scale=z_scales[h][:],
+                    start=True, stop=True,
+                )
+
+        units = [(0, 0, 512), (1, 0, 512), (2, 0, 512), (3, 0, 256), (3, 256, 512)]
+        members = [keep.tile([P, b - a, MEMBERS], F32, name=f"members{u}") for u, (c, a, b) in enumerate(units)]
+        sums = {}
+        roots = {}
+
+        def gather(u):
+            c, a, b = units[u]
+            if a == 0:
+                nc.scalar.activation(sq[c][:], s_ps[c][:], ACT.Square, scale=0.0625)
+            first, last = a // 4, b // 4
+            cut = first + 2 * ((last - first) * 5 // 16)
+            flat = members[u][:].rearrange("p g m -> p (g m)")
+            for lo, hi in column_pieces(first, cut, 30):
+                nc.scalar.activation(
+                    flat[:, 16 * (lo - first) : 16 * (hi - first)], sq[c][:].indirect(n3_t[:, lo:hi]), ACT.Copy
+                )
+            for lo, hi in column_pieces(cut, last, 30):
+                nc.vector.tensor_copy(flat[:, 16 * (lo - first) : 16 * (hi - first)], sq[c][:].indirect(n3_t[:, lo:hi]))
+
+        def add_pairs(u):
+            c, a, b = units[u]
+            pairs = keep.tile([P, b - a, 2], F32, name=f"pairs{u}")
+            nc.vector.tensor_tensor(pairs[:], members[u][:, :, 0:2], members[u][:, :, 2:4], ADD)
+            sums[u] = pairs
+
+        def root(u):
+            c, a, b = units[u]
+            total = keep.tile([P, b - a], F32, name=f"total{u}")
+            nc.vector.tensor_tensor(total[:], sums[u][:, :, 0], sums[u][:, :, 1], ADD)
+            inv = keep.tile([P, b - a], F32, name=f"inv{u}")
+            nc.scalar.activation(inv[:], total[:], ACT.Abs_reciprocal_sqrt, bias=0.5)
+            roots[u] = inv
+
+        def finish(u):
+            c, a, b = units[u]
+            res = keep.tile([P, b - a], F32, name=f"res{u}")
+            nc.vector.scalar_tensor_tensor(res[:], s_ps[c][:, a:b], 0.0625, roots[u][:], MULT, MULT)
+            nc.sync.dma_start(out[P * c : P * c + P, a:b], res[:])
+
+        n_units = len(units)
+        for step in range(n_units + 2):
+            if step < n_units:
+                gather(step)
+            if 0 <= step - 1 < n_units:
+                add_pairs(step - 1)
+            if 0 <= step - 2 < n_units:
+                finish(step - 2)
+            if 0 <= step - 1 < n_units:
+                root(step - 1)

@@ -15,183 +15,286 @@ FP8X4 = mybir.dt.float8_e4m3fn_x4
 ACT = mybir.ActivationFunctionType
 MULT = mybir.AluOpType.mult
 ADD = mybir.AluOpType.add
+SUBTRACT = mybir.AluOpType.subtract
 
 P = 128
 PACK = 4
 HALF = 256
+QUARTER = 128
 MEMBERS = 4
+S_SCALE = 0.0625
+ROOT_BIAS = 0.5
+LIST_COLUMN = 16
+MOST_LIST_COLUMNS = 30
+
+W_GROUPS_ON_SCALAR = 44
+TILES_ON_GPSIMD = 2
+WEAVE_ON_SCALAR = 160
+VECTOR_SHARE_EARLY = 34
+VECTOR_SHARE_LATE = 30
+VECTOR_SUMS_EVERY = 3
+FINISH_LAG = 5
 
 
-def column_pieces(first, last, most):
-    count = -(-(last - first) // most)
+def list_runs(first, last):
+    count = -(-(last - first) // MOST_LIST_COLUMNS)
     pairs = (last - first) // 2
     cuts = [first + 2 * (pairs * i // count) for i in range(count + 1)]
     return list(zip(cuts[:-1], cuts[1:]))
 
 
-def tile_picked_candehqgvar_none_p_kernel(tc, x_words, x_scales, w1, sl, th, gs, offs, n1, n2, cand, n3, out):
+def tile_picked_candehqgvar_none_p_kernel(
+    tc, x_words, x_scales, w1, sl, th, gs, offs, n1, n2, cand, n3, out
+):
     nc = tc.nc
+    halves = [slice(0, HALF), slice(HALF, S)]
+    list_halves = [slice(0, HALF // LIST_COLUMN), slice(HALF // LIST_COLUMN, S // LIST_COLUMN)]
+
     with ExitStack() as ctx:
         lists = ctx.enter_context(tc.tile_pool(name="lists", bufs=1))
         keep = ctx.enter_context(tc.tile_pool(name="keep", bufs=1))
         psum = ctx.enter_context(tc.psum_pool(name="psum", bufs=1))
 
-        offs_t = lists.tile([P, S // 16], U16, name="offs_t")
-        cand_t = lists.tile([P, C // 16], U16, name="cand_t")
-        n1_t = lists.tile([P, S // 16], U16, name="n1_t")
-        n2_t = lists.tile([P, S // 16], U16, name="n2_t")
-        n3_t = lists.tile([P, W // 16], U16, name="n3_t")
+        offs_list = lists.tile([P, S // LIST_COLUMN], U16, name="offs_list")
+        cand_list = lists.tile([P, C // LIST_COLUMN], U16, name="cand_list")
+        n1_list = lists.tile([P, S // LIST_COLUMN], U16, name="n1_list")
+        n2_list = lists.tile([P, S // LIST_COLUMN], U16, name="n2_list")
+        n3_list = lists.tile([P, W // LIST_COLUMN], U16, name="n3_list")
 
         table_scales = keep.tile([P, T], U8, name="table_scales", align_bytes=64)
         table_words = keep.tile([P, T], I32, name="table_words", align_bytes=64)
-        nc.vector.memset(table_scales[:].bitcast(I32), 0)
+        scale_rows = keep.tile([P, T // 4], I32, name="scale_rows", align_bytes=64)
+        nc.gpsimd.memset(table_scales[:].bitcast(I32), 0)
 
+        warm_sigmoid = keep.tile([P, 2], F32, name="warm_sigmoid")
+        nc.vector.memset(warm_sigmoid[:, 0:1], 0.0)
+        nc.scalar.activation(warm_sigmoid[:, 1:2], warm_sigmoid[:, 0:1], ACT.Sigmoid)
+
+        for q in range(4):
+            nc.sync.dma_start(scale_rows[32 * q : 32 * q + 4, :], x_scales[0, 4 * q : 4 * q + 4, :].bitcast(I32))
         w_rows = w1.rearrange("(p j) c -> p j c", j=PACK)
         w_raw = [keep.tile([P, PACK, HALF], F32, name=f"w_raw{h}", align_bytes=64) for h in range(2)]
-        nc.sync.dma_start(w_raw[0][:], w_rows[:, :, 0:HALF])
-        nc.sync.dma_start(offs_t[:], offs)
-        nc.sync.dma_start(cand_t[:], cand)
-        for q in range(4):
-            nc.sync.dma_start(
-                table_scales[32 * q : 32 * q + 4, :].bitcast(I32), x_scales[0, 4 * q : 4 * q + 4, :].bitcast(I32)
-            )
-        nc.sync.dma_start(w_raw[1][:], w_rows[:, :, HALF:H])
+        nc.sync.dma_start(offs_list[:], offs)
+        nc.sync.dma_start(w_raw[0][:], w_rows[:, :, halves[0]])
+        nc.sync.dma_start(cand_list[:], cand)
+        nc.sync.dma_start(w_raw[1][:], w_rows[:, :, halves[1]])
         nc.sync.dma_start(table_words[:], x_words[0].rearrange("p n t -> p (n t)").bitcast(I32))
-        nc.sync.dma_start(n1_t[:], n1)
-        nc.sync.dma_start(n2_t[:], n2)
-        nc.sync.dma_start(n3_t[:], n3)
+        for q in range(4):
+            nc.vector.tensor_copy(table_scales[32 * q : 32 * q + 4, :].bitcast(I32), scale_rows[32 * q : 32 * q + 4, :])
+        nc.sync.dma_start(n1_list[:], n1)
+        nc.sync.dma_start(n2_list[:], n2)
+        nc.sync.dma_start(n3_list[:], n3)
 
-        sl_t = keep.tile([P, PACK], F32, name="sl_t")
-        th_t = keep.tile([P, PACK], F32, name="th_t")
-        gs_t = keep.tile([P, PACK], F32, name="gs_t")
-        bias_t = keep.tile([P, PACK], F32, name="bias_t")
-        for tile, vec in ((sl_t, sl), (th_t, th), (gs_t, gs)):
-            nc.gpsimd.dma_start(tile[:], vec.rearrange("(p t) o -> p (t o)", t=PACK))
-        neg_sl = keep.tile([P, PACK], F32, name="neg_sl")
-        nc.gpsimd.tensor_scalar(neg_sl[:], sl_t[:], -1.0, 0.0, MULT, ADD)
-        nc.gpsimd.tensor_tensor(bias_t[:], neg_sl[:], th_t[:], MULT)
+        slope = keep.tile([P, PACK], F32, name="slope")
+        threshold = keep.tile([P, PACK], F32, name="threshold")
+        gain = keep.tile([P, PACK], F32, name="gain")
+        for row_values, source in ((slope, sl), (threshold, th), (gain, gs)):
+            nc.gpsimd.dma_start(row_values[:], source.rearrange("(p t) o -> p (t o)", t=PACK))
+        minus_slope = keep.tile([P, PACK], F32, name="minus_slope")
+        gate_bias = keep.tile([P, PACK], F32, name="gate_bias")
+        nc.gpsimd.tensor_scalar(minus_slope[:], slope[:], -1.0, 0.0, MULT, ADD)
+        nc.gpsimd.tensor_tensor(gate_bias[:], minus_slope[:], threshold[:], MULT)
 
-        q_scales = keep.tile([P, S], U8, name="q_scales", align_bytes=64)
-        c_scales = keep.tile([P, C], U8, name="c_scales", align_bytes=64)
-        q_words = keep.tile([P, S], U32, name="q_words", align_bytes=64)
-        c_words = keep.tile([P, C], U32, name="c_words", align_bytes=64)
-        nc.vector.tensor_copy(q_scales[:], table_scales[:].indirect(offs_t[:]))
-        nc.vector.tensor_copy(c_scales[:], table_scales[:].indirect(cand_t[:]))
+        token_scales = keep.tile([P, S], U8, name="token_scales", align_bytes=64)
+        token_words = keep.tile([P, S], U32, name="token_words", align_bytes=64)
+        cand_scales = keep.tile([P, C], U8, name="cand_scales", align_bytes=64)
+        cand_words = keep.tile([P, C], U32, name="cand_words", align_bytes=64)
+        nc.vector.tensor_copy(token_scales[:], table_scales[:].indirect(offs_list[:]))
 
         w_bf = keep.tile([P, PACK, P, PACK], BF16, name="w_bf", align_bytes=64)
-        for h in range(2):
-            nc.scalar.copy(
-                w_bf[:, :, 64 * h : 64 * h + 64, :].rearrange("p t m j -> p m j t"),
-                w_raw[h][:].rearrange("p j (m t) -> p m j t", t=PACK),
+        groups = HALF // PACK
+
+        def deal(h, first, last):
+            return (
+                w_bf[:, :, groups * h + first : groups * h + last, :].rearrange("p t m j -> p m t j"),
+                w_raw[h][:, :, PACK * first : PACK * last].rearrange("p j (m t) -> p m t j", t=PACK),
             )
+
+        nc.scalar.copy(*deal(0, 0, groups))
+        nc.scalar.copy(*deal(1, 0, W_GROUPS_ON_SCALAR))
+        nc.vector.tensor_copy(cand_scales[:], table_scales[:].indirect(cand_list[:]))
+        nc.vector.tensor_copy(*deal(1, W_GROUPS_ON_SCALAR, groups))
         w_codes = keep.tile([P, H], U32, name="w_codes", align_bytes=64)
         w_scales = keep.tile([P, H], U8, name="w_scales", align_bytes=64)
         nc.vector.quantize_mx(w_codes[:].bitcast(FP8X4), w_scales[:], w_bf[:].rearrange("p t m j -> p (t m j)"))
 
-        nc.vector.tensor_copy(q_words[:], table_words[:].bitcast(U32).indirect(offs_t[:]))
-        nc.vector.tensor_copy(c_words[:], table_words[:].bitcast(U32).indirect(cand_t[:]))
+        for h in range(2):
+            nc.vector.tensor_copy(
+                token_words[:, halves[h]], table_words[:].bitcast(U32).indirect(offs_list[:, list_halves[h]])
+            )
+        nc.vector.tensor_copy(cand_words[:], table_words[:].bitcast(U32).indirect(cand_list[:]))
 
-        y_ps = [psum.tile([P, S], F32, name=f"y_ps{t}") for t in range(PACK)]
-        y_sb = [keep.tile([P, S], F32, name=f"y_sb{t}") for t in range(PACK)]
-        y_neg = [keep.tile([P, S], F32, name=f"y_neg{t}") for t in range(PACK)]
+        y_first = psum.tile([P, HALF], F32, name="y_first", tag="bank4")
+        y_bank = [psum.tile([P, S], F32, name=f"y_bank{t}", tag=f"bank{t}") for t in range(PACK)]
+        y_half = [[y_bank[t][:, halves[h]] for h in range(2)] for t in range(PACK)]
+        y_half[0][0] = y_first[:]
+        minus_y = [keep.tile([P, S], F32, name=f"minus_y{t}") for t in range(PACK)]
+        minus_y_copy = [keep.tile([P, S], F32, name=f"minus_y_copy{t}", tag=f"reused{t}") for t in range(PACK)]
+
+        def project(t, target, cols):
+            rows = slice(P * t, P * t + P)
+            nc.tensor.matmul_mx(
+                target,
+                lhsT=w_codes[:, rows].bitcast(FP8X4),
+                lhsT_scale=w_scales[:, rows],
+                rhs=token_words[:, cols].bitcast(FP8X4),
+                rhs_scale=token_scales[:, cols],
+                start=True,
+                stop=True,
+            )
+            nc.scalar.activation(minus_y[t][:, cols], target, ACT.Copy, scale=-1.0)
+
+        for h in range(2):
+            project(0, y_half[0][h], halves[h])
+        for t in range(1, PACK):
+            project(t, y_bank[t][:], slice(0, S))
+        for t in (2, 3):
+            nc.sync.dma_start(minus_y_copy[t][:], minus_y[t][:])
+
         st = [keep.tile([P, S], F32, name=f"st{t}") for t in range(PACK)]
         sg = [keep.tile([P, S], F32, name=f"sg{t}") for t in range(PACK)]
-        z_f32 = [keep.tile([P, PACK, HALF], F32, name=f"z_f32{h}") for h in range(2)]
-        for t in range(PACK):
-            cols = slice(P * t, P * t + P)
-            nc.tensor.matmul_mx(
-                y_ps[t][:], lhsT=w_codes[:, cols].bitcast(FP8X4), lhsT_scale=w_scales[:, cols],
-                rhs=q_words[:].bitcast(FP8X4), rhs_scale=q_scales[:], start=True, stop=True,
+
+        def difference(t, h):
+            nc.vector.tensor_tensor(
+                st[t][:, halves[h]],
+                minus_y[t][:].indirect(n1_list[:, list_halves[h]]),
+                minus_y_copy[t][:, halves[h]],
+                SUBTRACT,
             )
-            nc.scalar.copy(y_sb[t][:], y_ps[t][:])
-        for t in range(PACK):
-            nc.vector.tensor_scalar(y_neg[t][:], y_sb[t][:], -1.0, None, MULT)
+
+        def gate(t):
             for h in range(2):
-                cols = slice(HALF * h, HALF * h + HALF)
-                nc.vector.tensor_tensor(
-                    st[t][:, cols], y_neg[t][:].indirect(n1_t[:, 16 * h : 16 * h + 16]), y_sb[t][:, cols], ADD
-                )
-            for h in range(2):
-                cols = slice(HALF * h, HALF * h + HALF)
                 nc.scalar.activation(
-                    sg[t][:, cols], st[t][:].indirect(n2_t[:, 16 * h : 16 * h + 16]), ACT.Sigmoid,
-                    bias=bias_t[:, t : t + 1], scale=sl_t[:, t : t + 1],
+                    sg[t][:, halves[h]],
+                    st[t][:].indirect(n2_list[:, list_halves[h]]),
+                    ACT.Sigmoid,
+                    bias=gate_bias[:, t : t + 1],
+                    scale=slope[:, t : t + 1],
                 )
-        z_codes = []
-        z_scales = []
+
+        weighted_y = [keep.tile([P, HALF], F32, name=f"weighted_y{t}") for t in range(TILES_ON_GPSIMD)]
+        for t in range(TILES_ON_GPSIMD):
+            nc.scalar.activation(weighted_y[t][:], y_half[t][1], ACT.Copy, scale=gain[:, t : t + 1])
+
+        nc.vector.tensor_copy(minus_y_copy[0][:], minus_y[0][:])
+        difference(0, 0)
+        nc.vector.tensor_copy(minus_y_copy[1][:], minus_y[1][:])
+        difference(0, 1)
+        gate(0)
+        for t in range(1, PACK):
+            for h in range(2):
+                difference(t, h)
+            gate(t)
+
+        z_f32 = [keep.tile([P, PACK, HALF], F32, name=f"z_f32{h}", tag=f"reused{2 + h}") for h in range(2)]
         for h in range(2):
-            cols = slice(HALF * h, HALF * h + HALF)
             for t in range(PACK):
-                nc.vector.scalar_tensor_tensor(
-                    z_f32[h][:, t, :], y_ps[t][:, cols], gs_t[:, t : t + 1], sg[t][:, cols], MULT, MULT
-                )
-            z_bf = keep.tile([P, HALF, PACK], BF16, name=f"z_bf{h}", align_bytes=64)
-            nc.vector.tensor_copy(
-                z_bf[:].rearrange("p (c i) t -> p c t i", i=4), z_f32[h][:].rearrange("p t (c i) -> p c t i", i=4)
+                if h == 1 and t < TILES_ON_GPSIMD:
+                    nc.gpsimd.tensor_tensor(z_f32[h][:, t, :], weighted_y[t][:], sg[t][:, halves[h]], MULT)
+                else:
+                    nc.vector.scalar_tensor_tensor(
+                        z_f32[h][:, t, :], y_half[t][h], gain[:, t : t + 1], sg[t][:, halves[h]], MULT, MULT
+                    )
+        z_bf = [keep.tile([P, HALF, PACK], BF16, name=f"z_bf{h}", align_bytes=64) for h in range(2)]
+        z_codes = keep.tile([P, S], U32, name="z_codes", align_bytes=64)
+        z_scales = keep.tile([P, S], U8, name="z_scales", align_bytes=64)
+
+        def weave(h, first, last):
+            return (
+                z_bf[h][:, first:last, :].rearrange("p (g i) t -> p g t i", i=4),
+                z_f32[h][:, :, first:last].rearrange("p t (g i) -> p g t i", i=4),
             )
-            codes = keep.tile([P, HALF], U32, name=f"z_codes{h}", align_bytes=64)
-            scales = keep.tile([P, HALF], U8, name=f"z_scales{h}", align_bytes=64)
-            nc.vector.quantize_mx(codes[:].bitcast(FP8X4), scales[:], z_bf[:].rearrange("p c t -> p (c t)"))
-            z_codes.append(codes)
-            z_scales.append(scales)
 
-        s_ps = [psum.tile([P, S], F32, name=f"s_ps{c}") for c in range(4)]
-        sq = [keep.tile([P, S], F32, name=f"sq{c}") for c in range(4)]
+        nc.scalar.copy(*weave(0, 0, WEAVE_ON_SCALAR))
+        warm_root = keep.tile([P, 1], F32, name="warm_root")
+        nc.scalar.activation(warm_root[:], z_bf[0][:, 0, 0:1], ACT.Abs_reciprocal_sqrt, bias=ROOT_BIAS)
+        nc.vector.tensor_copy(*weave(0, WEAVE_ON_SCALAR, HALF))
+        nc.vector.tensor_copy(*weave(1, 0, HALF))
         for h in range(2):
-            for c in range(4):
-                cols = slice(P * c, P * c + P)
-                nc.tensor.matmul_mx(
-                    s_ps[c][:, HALF * h : HALF * h + HALF], lhsT=c_words[:, cols].bitcast(FP8X4),
-                    lhsT_scale=c_scales[:, cols], rhs=z_codes[h][:].bitcast(FP8X4), rhs_scale=z_scales[h][:],
-                    start=True, stop=True,
+            nc.vector.quantize_mx(
+                z_codes[:, halves[h]].bitcast(FP8X4), z_scales[:, halves[h]], z_bf[h][:].rearrange("p j t -> p (j t)")
+            )
+
+        def score(c, target, cols):
+            rows = slice(P * c, P * c + P)
+            nc.tensor.matmul_mx(
+                target,
+                lhsT=cand_words[:, rows].bitcast(FP8X4),
+                lhsT_scale=cand_scales[:, rows],
+                rhs=z_codes[:, cols].bitcast(FP8X4),
+                rhs_scale=z_scales[:, cols],
+                start=True,
+                stop=True,
+            )
+
+        s_first = [psum.tile([P, HALF], F32, name=f"s_first{h}", tag=f"bank{4 * h}") for h in range(2)]
+        s_bank = {c: psum.tile([P, S], F32, name=f"s_bank{c}", tag=f"bank{4 + c}") for c in range(1, 4)}
+        for h in range(2):
+            score(0, s_first[h][:], halves[h])
+        for c in range(1, 4):
+            score(c, s_bank[c][:], slice(0, S))
+
+        def s_columns(c, first, last):
+            if c == 0:
+                return s_first[first // HALF][:, first % HALF : first % HALF + last - first]
+            return s_bank[c][:, first:last]
+
+        pieces = [(c, HALF * h, HALF * h + HALF) for c in range(4) for h in range(2)]
+        pieces = pieces[:-1] + [(3, HALF, HALF + QUARTER), (3, HALF + QUARTER, S)]
+        squares = [keep.tile([P, S], F32, name=f"squares{c}") for c in range(4)]
+        members = [keep.tile([P, b - a, MEMBERS], F32, name=f"members{u}") for u, (c, a, b) in enumerate(pieces)]
+        sums = [keep.tile([P, b - a], F32, name=f"sums{u}") for u, (c, a, b) in enumerate(pieces)]
+
+        def square(c, first, last):
+            nc.scalar.activation(squares[c][:, first:last], s_columns(c, first, last), ACT.Square, scale=S_SCALE)
+
+        def fetch(u):
+            c, a, b = pieces[u]
+            first, last = a * MEMBERS // LIST_COLUMN, b * MEMBERS // LIST_COLUMN
+            share = VECTOR_SHARE_EARLY if c < 2 else VECTOR_SHARE_LATE
+            cut = last - 2 * ((last - first) * share // 128)
+            entries = members[u][:].rearrange("p j t -> p (j t)")
+            for lo, hi in list_runs(cut, last):
+                nc.vector.tensor_copy(
+                    entries[:, LIST_COLUMN * (lo - first) : LIST_COLUMN * (hi - first)],
+                    squares[c][:].indirect(n3_list[:, lo:hi]),
                 )
-
-        units = [(0, 0, 512), (1, 0, 512), (2, 0, 512), (3, 0, 256), (3, 256, 512)]
-        members = [keep.tile([P, b - a, MEMBERS], F32, name=f"members{u}") for u, (c, a, b) in enumerate(units)]
-        sums = {}
-        roots = {}
-
-        def gather(u):
-            c, a, b = units[u]
-            if a == 0:
-                nc.scalar.activation(sq[c][:], s_ps[c][:], ACT.Square, scale=0.0625)
-            first, last = a // 4, b // 4
-            cut = first + 2 * ((last - first) * 5 // 16)
-            flat = members[u][:].rearrange("p g m -> p (g m)")
-            for lo, hi in column_pieces(first, cut, 30):
+            for lo, hi in list_runs(first, cut):
                 nc.scalar.activation(
-                    flat[:, 16 * (lo - first) : 16 * (hi - first)], sq[c][:].indirect(n3_t[:, lo:hi]), ACT.Copy
+                    entries[:, LIST_COLUMN * (lo - first) : LIST_COLUMN * (hi - first)],
+                    squares[c][:].indirect(n3_list[:, lo:hi]),
+                    ACT.Copy,
                 )
-            for lo, hi in column_pieces(cut, last, 30):
-                nc.vector.tensor_copy(flat[:, 16 * (lo - first) : 16 * (hi - first)], sq[c][:].indirect(n3_t[:, lo:hi]))
 
-        def add_pairs(u):
-            c, a, b = units[u]
+        def sum_on_gpsimd(u):
+            c, a, b = pieces[u]
             pairs = keep.tile([P, b - a, 2], F32, name=f"pairs{u}")
-            nc.vector.tensor_tensor(pairs[:], members[u][:, :, 0:2], members[u][:, :, 2:4], ADD)
-            sums[u] = pairs
+            nc.gpsimd.tensor_tensor(pairs[:], members[u][:, :, 0:2], members[u][:, :, 2:4], ADD)
+            nc.gpsimd.tensor_tensor(sums[u][:], pairs[:, :, 0], pairs[:, :, 1], ADD)
 
-        def root(u):
-            c, a, b = units[u]
-            total = keep.tile([P, b - a], F32, name=f"total{u}")
-            nc.vector.tensor_tensor(total[:], sums[u][:, :, 0], sums[u][:, :, 1], ADD)
-            inv = keep.tile([P, b - a], F32, name=f"inv{u}")
-            nc.scalar.activation(inv[:], total[:], ACT.Abs_reciprocal_sqrt, bias=0.5)
-            roots[u] = inv
+        def sum_on_vector(u):
+            nc.vector.tensor_reduce(sums[u][:], members[u][:], mybir.AxisListType.X, ADD)
 
         def finish(u):
-            c, a, b = units[u]
-            res = keep.tile([P, b - a], F32, name=f"res{u}")
-            nc.vector.scalar_tensor_tensor(res[:], s_ps[c][:, a:b], 0.0625, roots[u][:], MULT, MULT)
-            nc.sync.dma_start(out[P * c : P * c + P, a:b], res[:])
+            c, a, b = pieces[u]
+            inverse_root = keep.tile([P, b - a], F32, name=f"inverse_root{u}")
+            nc.scalar.activation(inverse_root[:], sums[u][:], ACT.Abs_reciprocal_sqrt, bias=ROOT_BIAS)
+            result = keep.tile([P, b - a], F32, name=f"result{u}")
+            nc.vector.scalar_tensor_tensor(result[:], s_columns(c, a, b), S_SCALE, inverse_root[:], MULT, MULT)
+            nc.sync.dma_start(out[P * c : P * c + P, a:b], result[:])
 
-        n_units = len(units)
-        for step in range(n_units + 2):
-            if step < n_units:
-                gather(step)
-            if 0 <= step - 1 < n_units:
-                add_pairs(step - 1)
-            if 0 <= step - 2 < n_units:
-                finish(step - 2)
-            if 0 <= step - 1 < n_units:
-                root(step - 1)
+        on_vector = [u for u in range(len(pieces)) if u % VECTOR_SUMS_EVERY == VECTOR_SUMS_EVERY - 1]
+        for h in range(2):
+            square(0, HALF * h, HALF * h + HALF)
+        for step in range(len(pieces) + FINISH_LAG):
+            if step < len(pieces):
+                fetch(step)
+                if step not in on_vector:
+                    sum_on_gpsimd(step)
+                c, a, b = pieces[step]
+                if a == 0 and c < 3:
+                    square(c + 1, 0, S)
+            if step - 1 in on_vector:
+                sum_on_vector(step - 1)
+            if step >= FINISH_LAG:
+                finish(step - FINISH_LAG)

@@ -1,6 +1,7 @@
 from contextlib import ExitStack
 
 import concourse.mybir as mybir
+from concourse.masks import make_identity
 
 K, T, S, H, C, W = 512, 2048, 512, 512, 512, 2048
 FLOPS = 2 * K * H * S + 2 * K * C * S
@@ -25,22 +26,14 @@ MEMBERS = 4
 S_SCALE = 0.0625
 ROOT_BIAS = 0.5
 LIST_COLUMN = 16
-MOST_LIST_COLUMNS = 30
 
 W_GROUPS_ON_SCALAR = 44
 TILES_ON_GPSIMD = 2
 WEAVE_ON_SCALAR = 160
-VECTOR_SHARE_EARLY = 34
-VECTOR_SHARE_LATE = 30
-VECTOR_SUMS_EVERY = 3
+VECTOR_SHARE_EARLY = 36
+VECTOR_SHARE_LATE = 34
+TENSOR_SUMS_EVERY = 3
 FINISH_LAG = 5
-
-
-def list_runs(first, last):
-    count = -(-(last - first) // MOST_LIST_COLUMNS)
-    pairs = (last - first) // 2
-    cuts = [first + 2 * (pairs * i // count) for i in range(count + 1)]
-    return list(zip(cuts[:-1], cuts[1:]))
 
 
 def tile_picked_candehqgvar_none_p_kernel(
@@ -94,6 +87,9 @@ def tile_picked_candehqgvar_none_p_kernel(
         gate_bias = keep.tile([P, PACK], F32, name="gate_bias")
         nc.gpsimd.tensor_scalar(minus_slope[:], slope[:], -1.0, 0.0, MULT, ADD)
         nc.gpsimd.tensor_tensor(gate_bias[:], minus_slope[:], threshold[:], MULT)
+
+        identity = keep.tile([P, P], F32, name="identity")
+        make_identity(nc, identity[:])
 
         token_scales = keep.tile([P, S], U8, name="token_scales", align_bytes=64)
         token_words = keep.tile([P, S], U32, name="token_words", align_bytes=64)
@@ -152,7 +148,8 @@ def tile_picked_candehqgvar_none_p_kernel(
             nc.sync.dma_start(minus_y_copy[t][:], minus_y[t][:])
 
         st = [keep.tile([P, S], F32, name=f"st{t}") for t in range(PACK)]
-        sg = [keep.tile([P, S], F32, name=f"sg{t}") for t in range(PACK)]
+        squares = [keep.tile([P, 2 * S], F32, name=f"squares{t}") for t in range(PACK)]
+        sg = [squares[t][:, S : 2 * S] for t in range(PACK)]
 
         def difference(t, h):
             nc.vector.tensor_tensor(
@@ -207,7 +204,7 @@ def tile_picked_candehqgvar_none_p_kernel(
 
         nc.scalar.copy(*weave(0, 0, WEAVE_ON_SCALAR))
         warm_root = keep.tile([P, 1], F32, name="warm_root")
-        nc.scalar.activation(warm_root[:], z_bf[0][:, 0, 0:1], ACT.Abs_reciprocal_sqrt, bias=ROOT_BIAS)
+        nc.scalar.activation(warm_root[:], z_bf[0][:, 0, 0:1], ACT.Abs_reciprocal_sqrt, bias=ROOT_BIAS, scale=0.0)
         nc.vector.tensor_copy(*weave(0, WEAVE_ON_SCALAR, HALF))
         nc.vector.tensor_copy(*weave(1, 0, HALF))
         for h in range(2):
@@ -241,9 +238,10 @@ def tile_picked_candehqgvar_none_p_kernel(
 
         pieces = [(c, HALF * h, HALF * h + HALF) for c in range(4) for h in range(2)]
         pieces = pieces[:-1] + [(3, HALF, HALF + QUARTER), (3, HALF + QUARTER, S)]
-        squares = [keep.tile([P, S], F32, name=f"squares{c}") for c in range(4)]
+        last_piece = len(pieces) - 1
+        on_tensor = range(0, last_piece, TENSOR_SUMS_EVERY)
         members = [keep.tile([P, b - a, MEMBERS], F32, name=f"members{u}") for u, (c, a, b) in enumerate(pieces)]
-        sums = [keep.tile([P, b - a], F32, name=f"sums{u}") for u, (c, a, b) in enumerate(pieces)]
+        sums = {}
 
         def square(c, first, last):
             nc.scalar.activation(squares[c][:, first:last], s_columns(c, first, last), ACT.Square, scale=S_SCALE)
@@ -254,47 +252,68 @@ def tile_picked_candehqgvar_none_p_kernel(
             share = VECTOR_SHARE_EARLY if c < 2 else VECTOR_SHARE_LATE
             cut = last - 2 * ((last - first) * share // 128)
             entries = members[u][:].rearrange("p j t -> p (j t)")
-            for lo, hi in list_runs(cut, last):
-                nc.vector.tensor_copy(
-                    entries[:, LIST_COLUMN * (lo - first) : LIST_COLUMN * (hi - first)],
-                    squares[c][:].indirect(n3_list[:, lo:hi]),
-                )
-            for lo, hi in list_runs(first, cut):
-                nc.scalar.activation(
-                    entries[:, LIST_COLUMN * (lo - first) : LIST_COLUMN * (hi - first)],
-                    squares[c][:].indirect(n3_list[:, lo:hi]),
-                    ACT.Copy,
-                )
+            on_scalar = LIST_COLUMN * (cut - first)
+            nc.vector.tensor_copy(entries[:, on_scalar:], squares[c][:].indirect(n3_list[:, cut:last]))
+            nc.scalar.activation(entries[:, :on_scalar], squares[c][:].indirect(n3_list[:, first:cut]), ACT.Copy)
 
         def sum_on_gpsimd(u):
             c, a, b = pieces[u]
             pairs = keep.tile([P, b - a, 2], F32, name=f"pairs{u}")
+            sums[u] = keep.tile([P, b - a], F32, name=f"sums{u}")
             nc.gpsimd.tensor_tensor(pairs[:], members[u][:, :, 0:2], members[u][:, :, 2:4], ADD)
             nc.gpsimd.tensor_tensor(sums[u][:], pairs[:, :, 0], pairs[:, :, 1], ADD)
 
         def sum_on_vector(u):
+            c, a, b = pieces[u]
+            sums[u] = keep.tile([P, b - a], F32, name=f"sums{u}")
             nc.vector.tensor_reduce(sums[u][:], members[u][:], mybir.AxisListType.X, ADD)
+
+        def sum_on_tensor(u):
+            c, a, b = pieces[u]
+            bank = 1 + 2 * (u // TENSOR_SUMS_EVERY % 2)
+            sums[u] = psum.tile([P, b - a], F32, name=f"turned_sums{u}", tag=f"bank{bank}")
+            for first in range(0, b - a, P):
+                for t in range(MEMBERS):
+                    nc.tensor.matmul(
+                        sums[u][:, first : first + P],
+                        members[u][:, first : first + P, t],
+                        identity[:],
+                        start=t == 0,
+                        stop=t == MEMBERS - 1,
+                        is_transpose=True,
+                    )
 
         def finish(u):
             c, a, b = pieces[u]
             inverse_root = keep.tile([P, b - a], F32, name=f"inverse_root{u}")
-            nc.scalar.activation(inverse_root[:], sums[u][:], ACT.Abs_reciprocal_sqrt, bias=ROOT_BIAS)
             result = keep.tile([P, b - a], F32, name=f"result{u}")
-            nc.vector.scalar_tensor_tensor(result[:], s_columns(c, a, b), S_SCALE, inverse_root[:], MULT, MULT)
+            if u in on_tensor:
+                s_copy = keep.tile([P, b - a], F32, name=f"s_copy{u}")
+                nc.vector.tensor_copy(s_copy[:], s_columns(c, a, b))
+                nc.scalar.activation(inverse_root[:], sums[u][:], ACT.Abs_reciprocal_sqrt, bias=ROOT_BIAS)
+                bank = 2 * (1 - u // TENSOR_SUMS_EVERY % 2)
+                turned_back = psum.tile([P, b - a], F32, name=f"turned_back{u}", tag=f"bank{bank}")
+                for first in range(0, b - a, P):
+                    nc.tensor.transpose(turned_back[:, first : first + P], inverse_root[:, first : first + P], identity[:])
+                nc.vector.scalar_tensor_tensor(result[:], turned_back[:], S_SCALE, s_copy[:], MULT, MULT)
+            else:
+                nc.scalar.activation(inverse_root[:], sums[u][:], ACT.Abs_reciprocal_sqrt, bias=ROOT_BIAS)
+                nc.vector.scalar_tensor_tensor(result[:], s_columns(c, a, b), S_SCALE, inverse_root[:], MULT, MULT)
             nc.sync.dma_start(out[P * c : P * c + P, a:b], result[:])
 
-        on_vector = [u for u in range(len(pieces)) if u % VECTOR_SUMS_EVERY == VECTOR_SUMS_EVERY - 1]
         for h in range(2):
             square(0, HALF * h, HALF * h + HALF)
         for step in range(len(pieces) + FINISH_LAG):
             if step < len(pieces):
                 fetch(step)
-                if step not in on_vector:
+                if step in on_tensor:
+                    sum_on_tensor(step)
+                elif step != last_piece:
                     sum_on_gpsimd(step)
                 c, a, b = pieces[step]
                 if a == 0 and c < 3:
                     square(c + 1, 0, S)
-            if step - 1 in on_vector:
-                sum_on_vector(step - 1)
+            if step == last_piece + 1:
+                sum_on_vector(last_piece)
             if step >= FINISH_LAG:
                 finish(step - FINISH_LAG)

from contextlib import ExitStack

import concourse.mybir as mybir
from concourse.masks import make_identity

K, T, S, H, C, W = 512, 2048, 512, 512, 512, 2048
FLOPS = 2 * K * H * S + 2 * K * C * S

F32 = mybir.dt.float32
BF16 = mybir.dt.bfloat16
I32 = mybir.dt.int32
U32 = mybir.dt.uint32
U16 = mybir.dt.uint16
U8 = mybir.dt.uint8
FP8X4 = mybir.dt.float8_e4m3fn_x4
ACT = mybir.ActivationFunctionType
MULT = mybir.AluOpType.mult
ADD = mybir.AluOpType.add
SUBTRACT = mybir.AluOpType.subtract

P = 128
PACK = 4
HALF = 256
QUARTER = 128
MEMBERS = 4
S_SCALE = 0.0625
ROOT_BIAS = 0.5
LIST_COLUMN = 16

W_GROUPS_ON_SCALAR = 44
TILES_ON_GPSIMD = 2
WEAVE_ON_SCALAR = 160
VECTOR_SHARE_EARLY = 36
VECTOR_SHARE_LATE = 34
TENSOR_SUMS_EVERY = 3
FINISH_LAG = 5


def tile_picked_candehqgvar_none_p_kernel(
    tc, x_words, x_scales, w1, sl, th, gs, offs, n1, n2, cand, n3, out
):
    nc = tc.nc
    halves = [slice(0, HALF), slice(HALF, S)]
    list_halves = [slice(0, HALF // LIST_COLUMN), slice(HALF // LIST_COLUMN, S // LIST_COLUMN)]

    with ExitStack() as ctx:
        lists = ctx.enter_context(tc.tile_pool(name="lists", bufs=1))
        keep = ctx.enter_context(tc.tile_pool(name="keep", bufs=1))
        psum = ctx.enter_context(tc.psum_pool(name="psum", bufs=1))

        offs_list = lists.tile([P, S // LIST_COLUMN], U16, name="offs_list")
        cand_list = lists.tile([P, C // LIST_COLUMN], U16, name="cand_list")
        n1_list = lists.tile([P, S // LIST_COLUMN], U16, name="n1_list")
        n2_list = lists.tile([P, S // LIST_COLUMN], U16, name="n2_list")
        n3_list = lists.tile([P, W // LIST_COLUMN], U16, name="n3_list")

        table_scales = keep.tile([P, T], U8, name="table_scales", align_bytes=64)
        table_words = keep.tile([P, T], I32, name="table_words", align_bytes=64)
        scale_rows = keep.tile([P, T // 4], I32, name="scale_rows", align_bytes=64)
        nc.gpsimd.memset(table_scales[:].bitcast(I32), 0)

        warm_sigmoid = keep.tile([P, 2], F32, name="warm_sigmoid")
        nc.vector.memset(warm_sigmoid[:, 0:1], 0.0)
        nc.scalar.activation(warm_sigmoid[:, 1:2], warm_sigmoid[:, 0:1], ACT.Sigmoid)

        for q in range(4):
            nc.sync.dma_start(scale_rows[32 * q : 32 * q + 4, :], x_scales[0, 4 * q : 4 * q + 4, :].bitcast(I32))
        w_rows = w1.rearrange("(p j) c -> p j c", j=PACK)
        w_raw = [keep.tile([P, PACK, HALF], F32, name=f"w_raw{h}", align_bytes=64) for h in range(2)]
        nc.sync.dma_start(offs_list[:], offs)
        nc.sync.dma_start(w_raw[0][:], w_rows[:, :, halves[0]])
        nc.sync.dma_start(cand_list[:], cand)
        nc.sync.dma_start(w_raw[1][:], w_rows[:, :, halves[1]])
        nc.sync.dma_start(table_words[:], x_words[0].rearrange("p n t -> p (n t)").bitcast(I32))
        for q in range(4):
            nc.vector.tensor_copy(table_scales[32 * q : 32 * q + 4, :].bitcast(I32), scale_rows[32 * q : 32 * q + 4, :])
        nc.sync.dma_start(n1_list[:], n1)
        nc.sync.dma_start(n2_list[:], n2)
        nc.sync.dma_start(n3_list[:], n3)

        slope = keep.tile([P, PACK], F32, name="slope")
        threshold = keep.tile([P, PACK], F32, name="threshold")
        gain = keep.tile([P, PACK], F32, name="gain")
        for row_values, source in ((slope, sl), (threshold, th), (gain, gs)):
            nc.gpsimd.dma_start(row_values[:], source.rearrange("(p t) o -> p (t o)", t=PACK))
        minus_slope = keep.tile([P, PACK], F32, name="minus_slope")
        gate_bias = keep.tile([P, PACK], F32, name="gate_bias")
        nc.gpsimd.tensor_scalar(minus_slope[:], slope[:], -1.0, 0.0, MULT, ADD)
        nc.gpsimd.tensor_tensor(gate_bias[:], minus_slope[:], threshold[:], MULT)

        identity = keep.tile([P, P], F32, name="identity")
        make_identity(nc, identity[:])

        token_scales = keep.tile([P, S], U8, name="token_scales", align_bytes=64)
        token_words = keep.tile([P, S], U32, name="token_words", align_bytes=64)
        cand_scales = keep.tile([P, C], U8, name="cand_scales", align_bytes=64)
        cand_words = keep.tile([P, C], U32, name="cand_words", align_bytes=64)
        nc.vector.tensor_copy(token_scales[:], table_scales[:].indirect(offs_list[:]))

        w_bf = keep.tile([P, PACK, P, PACK], BF16, name="w_bf", align_bytes=64)
        groups = HALF // PACK

        def deal(h, first, last):
            return (
                w_bf[:, :, groups * h + first : groups * h + last, :].rearrange("p t m j -> p m t j"),
                w_raw[h][:, :, PACK * first : PACK * last].rearrange("p j (m t) -> p m t j", t=PACK),
            )

        nc.scalar.copy(*deal(0, 0, groups))
        nc.scalar.copy(*deal(1, 0, W_GROUPS_ON_SCALAR))
        nc.vector.tensor_copy(cand_scales[:], table_scales[:].indirect(cand_list[:]))
        nc.vector.tensor_copy(*deal(1, W_GROUPS_ON_SCALAR, groups))
        w_codes = keep.tile([P, H], U32, name="w_codes", align_bytes=64)
        w_scales = keep.tile([P, H], U8, name="w_scales", align_bytes=64)
        nc.vector.quantize_mx(w_codes[:].bitcast(FP8X4), w_scales[:], w_bf[:].rearrange("p t m j -> p (t m j)"))

        for h in range(2):
            nc.vector.tensor_copy(
                token_words[:, halves[h]], table_words[:].bitcast(U32).indirect(offs_list[:, list_halves[h]])
            )
        nc.vector.tensor_copy(cand_words[:], table_words[:].bitcast(U32).indirect(cand_list[:]))

        y_first = psum.tile([P, HALF], F32, name="y_first", tag="bank4")
        y_bank = [psum.tile([P, S], F32, name=f"y_bank{t}", tag=f"bank{t}") for t in range(PACK)]
        y_half = [[y_bank[t][:, halves[h]] for h in range(2)] for t in range(PACK)]
        y_half[0][0] = y_first[:]
        minus_y = [keep.tile([P, S], F32, name=f"minus_y{t}") for t in range(PACK)]
        minus_y_copy = [keep.tile([P, S], F32, name=f"minus_y_copy{t}", tag=f"reused{t}") for t in range(PACK)]

        def project(t, target, cols):
            rows = slice(P * t, P * t + P)
            nc.tensor.matmul_mx(
                target,
                lhsT=w_codes[:, rows].bitcast(FP8X4),
                lhsT_scale=w_scales[:, rows],
                rhs=token_words[:, cols].bitcast(FP8X4),
                rhs_scale=token_scales[:, cols],
                start=True,
                stop=True,
            )
            nc.scalar.activation(minus_y[t][:, cols], target, ACT.Copy, scale=-1.0)

        for h in range(2):
            project(0, y_half[0][h], halves[h])
        for t in range(1, PACK):
            project(t, y_bank[t][:], slice(0, S))
        for t in (2, 3):
            nc.sync.dma_start(minus_y_copy[t][:], minus_y[t][:])

        st = [keep.tile([P, S], F32, name=f"st{t}") for t in range(PACK)]
        squares = [keep.tile([P, 2 * S], F32, name=f"squares{t}") for t in range(PACK)]
        sg = [squares[t][:, S : 2 * S] for t in range(PACK)]

        def difference(t, h):
            nc.vector.tensor_tensor(
                st[t][:, halves[h]],
                minus_y[t][:].indirect(n1_list[:, list_halves[h]]),
                minus_y_copy[t][:, halves[h]],
                SUBTRACT,
            )

        def gate(t):
            for h in range(2):
                nc.scalar.activation(
                    sg[t][:, halves[h]],
                    st[t][:].indirect(n2_list[:, list_halves[h]]),
                    ACT.Sigmoid,
                    bias=gate_bias[:, t : t + 1],
                    scale=slope[:, t : t + 1],
                )

        weighted_y = [keep.tile([P, HALF], F32, name=f"weighted_y{t}") for t in range(TILES_ON_GPSIMD)]
        for t in range(TILES_ON_GPSIMD):
            nc.scalar.activation(weighted_y[t][:], y_half[t][1], ACT.Copy, scale=gain[:, t : t + 1])

        nc.vector.tensor_copy(minus_y_copy[0][:], minus_y[0][:])
        difference(0, 0)
        nc.vector.tensor_copy(minus_y_copy[1][:], minus_y[1][:])
        difference(0, 1)
        gate(0)
        for t in range(1, PACK):
            for h in range(2):
                difference(t, h)
            gate(t)

        z_f32 = [keep.tile([P, PACK, HALF], F32, name=f"z_f32{h}", tag=f"reused{2 + h}") for h in range(2)]
        for h in range(2):
            for t in range(PACK):
                if h == 1 and t < TILES_ON_GPSIMD:
                    nc.gpsimd.tensor_tensor(z_f32[h][:, t, :], weighted_y[t][:], sg[t][:, halves[h]], MULT)
                else:
                    nc.vector.scalar_tensor_tensor(
                        z_f32[h][:, t, :], y_half[t][h], gain[:, t : t + 1], sg[t][:, halves[h]], MULT, MULT
                    )
        z_bf = [keep.tile([P, HALF, PACK], BF16, name=f"z_bf{h}", align_bytes=64) for h in range(2)]
        z_codes = keep.tile([P, S], U32, name="z_codes", align_bytes=64)
        z_scales = keep.tile([P, S], U8, name="z_scales", align_bytes=64)

        def weave(h, first, last):
            return (
                z_bf[h][:, first:last, :].rearrange("p (g i) t -> p g t i", i=4),
                z_f32[h][:, :, first:last].rearrange("p t (g i) -> p g t i", i=4),
            )

        nc.scalar.copy(*weave(0, 0, WEAVE_ON_SCALAR))
        warm_root = keep.tile([P, 1], F32, name="warm_root")
        nc.scalar.activation(warm_root[:], z_bf[0][:, 0, 0:1], ACT.Abs_reciprocal_sqrt, bias=ROOT_BIAS, scale=0.0)
        nc.vector.tensor_copy(*weave(0, WEAVE_ON_SCALAR, HALF))
        nc.vector.tensor_copy(*weave(1, 0, HALF))
        for h in range(2):
            nc.vector.quantize_mx(
                z_codes[:, halves[h]].bitcast(FP8X4), z_scales[:, halves[h]], z_bf[h][:].rearrange("p j t -> p (j t)")
            )

        def score(c, target, cols):
            rows = slice(P * c, P * c + P)
            nc.tensor.matmul_mx(
                target,
                lhsT=cand_words[:, rows].bitcast(FP8X4),
                lhsT_scale=cand_scales[:, rows],
                rhs=z_codes[:, cols].bitcast(FP8X4),
                rhs_scale=z_scales[:, cols],
                start=True,
                stop=True,
            )

        s_first = [psum.tile([P, HALF], F32, name=f"s_first{h}", tag=f"bank{4 * h}") for h in range(2)]
        s_bank = {c: psum.tile([P, S], F32, name=f"s_bank{c}", tag=f"bank{4 + c}") for c in range(1, 4)}
        for h in range(2):
            score(0, s_first[h][:], halves[h])
        for c in range(1, 4):
            score(c, s_bank[c][:], slice(0, S))

        def s_columns(c, first, last):
            if c == 0:
                return s_first[first // HALF][:, first % HALF : first % HALF + last - first]
            return s_bank[c][:, first:last]

        pieces = [(c, HALF * h, HALF * h + HALF) for c in range(4) for h in range(2)]
        pieces = pieces[:-1] + [(3, HALF, HALF + QUARTER), (3, HALF + QUARTER, S)]
        last_piece = len(pieces) - 1
        on_tensor = range(0, last_piece, TENSOR_SUMS_EVERY)
        members = [keep.tile([P, b - a, MEMBERS], F32, name=f"members{u}") for u, (c, a, b) in enumerate(pieces)]
        sums = {}

        def square(c, first, last):
            nc.scalar.activation(squares[c][:, first:last], s_columns(c, first, last), ACT.Square, scale=S_SCALE)

        def fetch(u):
            c, a, b = pieces[u]
            first, last = a * MEMBERS // LIST_COLUMN, b * MEMBERS // LIST_COLUMN
            share = VECTOR_SHARE_EARLY if c < 2 else VECTOR_SHARE_LATE
            cut = last - 2 * ((last - first) * share // 128)
            entries = members[u][:].rearrange("p j t -> p (j t)")
            on_scalar = LIST_COLUMN * (cut - first)
            nc.vector.tensor_copy(entries[:, on_scalar:], squares[c][:].indirect(n3_list[:, cut:last]))
            nc.scalar.activation(entries[:, :on_scalar], squares[c][:].indirect(n3_list[:, first:cut]), ACT.Copy)

        def sum_on_gpsimd(u):
            c, a, b = pieces[u]
            pairs = keep.tile([P, b - a, 2], F32, name=f"pairs{u}")
            sums[u] = keep.tile([P, b - a], F32, name=f"sums{u}")
            nc.gpsimd.tensor_tensor(pairs[:], members[u][:, :, 0:2], members[u][:, :, 2:4], ADD)
            nc.gpsimd.tensor_tensor(sums[u][:], pairs[:, :, 0], pairs[:, :, 1], ADD)

        def sum_on_vector(u):
            c, a, b = pieces[u]
            sums[u] = keep.tile([P, b - a], F32, name=f"sums{u}")
            nc.vector.tensor_reduce(sums[u][:], members[u][:], mybir.AxisListType.X, ADD)

        def sum_on_tensor(u):
            c, a, b = pieces[u]
            bank = 1 + 2 * (u // TENSOR_SUMS_EVERY % 2)
            sums[u] = psum.tile([P, b - a], F32, name=f"turned_sums{u}", tag=f"bank{bank}")
            for first in range(0, b - a, P):
                for t in range(MEMBERS):
                    nc.tensor.matmul(
                        sums[u][:, first : first + P],
                        members[u][:, first : first + P, t],
                        identity[:],
                        start=t == 0,
                        stop=t == MEMBERS - 1,
                        is_transpose=True,
                    )

        def finish(u):
            c, a, b = pieces[u]
            inverse_root = keep.tile([P, b - a], F32, name=f"inverse_root{u}")
            result = keep.tile([P, b - a], F32, name=f"result{u}")
            if u in on_tensor:
                s_copy = keep.tile([P, b - a], F32, name=f"s_copy{u}")
                nc.vector.tensor_copy(s_copy[:], s_columns(c, a, b))
                nc.scalar.activation(inverse_root[:], sums[u][:], ACT.Abs_reciprocal_sqrt, bias=ROOT_BIAS)
                bank = 2 * (1 - u // TENSOR_SUMS_EVERY % 2)
                turned_back = psum.tile([P, b - a], F32, name=f"turned_back{u}", tag=f"bank{bank}")
                for first in range(0, b - a, P):
                    nc.tensor.transpose(turned_back[:, first : first + P], inverse_root[:, first : first + P], identity[:])
                nc.vector.scalar_tensor_tensor(result[:], turned_back[:], S_SCALE, s_copy[:], MULT, MULT)
            else:
                nc.scalar.activation(inverse_root[:], sums[u][:], ACT.Abs_reciprocal_sqrt, bias=ROOT_BIAS)
                nc.vector.scalar_tensor_tensor(result[:], s_columns(c, a, b), S_SCALE, inverse_root[:], MULT, MULT)
            nc.sync.dma_start(out[P * c : P * c + P, a:b], result[:])

        for h in range(2):
            square(0, HALF * h, HALF * h + HALF)
        for step in range(len(pieces) + FINISH_LAG):
            if step < len(pieces):
                fetch(step)
                if step in on_tensor:
                    sum_on_tensor(step)
                elif step != last_piece:
                    sum_on_gpsimd(step)
                c, a, b = pieces[step]
                if a == 0 and c < 3:
                    square(c + 1, 0, S)
            if step == last_piece + 1:
                sum_on_vector(last_piece)
            if step >= FINISH_LAG:
                finish(step - FINISH_LAG)
